import numpy as np
import ml_dtypes


def mxq(x, axis, fmt="e4m3"):
    dtype, down = {"e4m3": (ml_dtypes.float8_e4m3fn, 7), "e5m2": (ml_dtypes.float8_e5m2, 14)}[fmt]
    v = np.moveaxis(np.asarray(x, np.float32).astype(ml_dtypes.bfloat16).astype(np.float64), axis, -1)
    blocks = v.reshape(v.shape[:-1] + (-1, 32))
    amax = np.abs(blocks).max(-1, keepdims=True)
    byte = np.maximum(np.where(amax > 0, np.frexp(amax)[1] - 1 + 127, 0) - down, 1)
    scale = np.exp2(byte - 127.0)
    codes = (blocks / scale).astype(np.float32).astype(dtype).astype(np.float64)
    return np.moveaxis((codes * scale).reshape(v.shape), -1, axis)


WIDE = False


def mx_kscale(k):
    if not WIDE:
        return np.ones(k)
    levels = np.array([30, -30])
    if k % 512:
        return np.exp2(np.random.permutation(np.resize(levels, k // 32))).repeat(32)
    a = np.empty((k // 512, 16))
    for p in range(k // 512):
        a[p, :8] = np.random.permutation(np.resize(levels, 8))
        for g in range(8):
            far = levels[np.abs(levels - a[p, g]) >= 10]
            a[p, g + 8] = far[np.random.randint(len(far))]
    return np.exp2(a.ravel()).repeat(32)


def f64(x):
    return np.asarray(x).astype(np.float64)


def striped(idx):
    return np.tile(np.asarray(idx).reshape(-1, 16).T, (8, 1)).astype(np.uint16)


def unstriped(offs):
    return offs[:16].T.reshape(-1).astype(np.int64)


E2M1 = np.array([0.0, 0.5, 1.0, 1.5, 2.0, 3.0, 4.0, 6.0, -0.0, -0.5, -1.0, -1.5, -2.0, -3.0, -4.0, -6.0])


def pack_weight(w, fmt):
    k, n = w.shape
    w = f64(np.asarray(w, np.float32).astype(ml_dtypes.bfloat16)).reshape(k // 32, 32, n)
    amax = np.abs(w).max(1)
    if fmt == "e4m3":
        byte = np.frexp(amax)[1] - 1 + 127 - 7
    else:
        mant, ex = np.frexp(amax / 6.0)
        byte = np.where(mant > 0.5, ex, ex - 1) + 127
    byte = np.clip(np.where(amax > 0, byte, 1), 1, 254)
    scaled = (w * np.exp2(127.0 - byte)[:, None, :]).reshape(k, n).astype(np.float32)
    by_word = np.ascontiguousarray(scaled.reshape(k // 512, 128, 4, n).transpose(0, 1, 3, 2))
    if fmt == "e4m3":
        words = by_word.astype(ml_dtypes.float8_e4m3fn).view(np.uint8)
    else:
        c = by_word.astype(ml_dtypes.float4_e2m1fn).view(np.uint8) & 0xF
        words = (c[..., 0::2] | (c[..., 1::2] << 4)).reshape(k // 512, 128, 2 * n)
    return np.ascontiguousarray(words), np.ascontiguousarray(byte.astype(np.uint8).reshape(k // 512, 16, n))


def unpack_weight(words, scales, fmt):
    g, _, n = scales.shape
    words = np.ascontiguousarray(words).reshape(g, 128, n, -1)
    if fmt == "e4m3":
        vals = words.view(ml_dtypes.float8_e4m3fn).astype(np.float64)
    else:
        nib = np.empty((g, 128, n, 4), np.uint8)
        nib[..., 0::2] = words & 0xF
        nib[..., 1::2] = words >> 4
        vals = E2M1[nib]
    vals = vals * np.repeat(np.exp2(scales.astype(np.float64) - 127.0), 8, axis=1)[..., None]
    return vals.transpose(0, 1, 3, 2).reshape(g * 512, n)


K, T, J, R, N = 512, 512, 256, 512, 256


def setup_inputs():
    n = np.random.standard_normal
    idx = np.random.permutation(T)[:J]
    idx2 = np.random.permutation(T)[:J]
    fk = mx_kscale(K)
    fr = mx_kscale(R)
    wp = pack_weight(n((K, R)) * 1 / np.sqrt(K) * fk[:, None], "e2m1")
    wbp = pack_weight(n((R, N)) * 1 / np.sqrt(R) / fr[:, None], "e4m3")
    return {
        "xf": (n((K, T))).astype(np.float32),
        "fk": (np.random.uniform(0.5, 2.0, (K, 1)) / fk[:, None]).astype(np.float32),
        "w_words": wp[0],
        "w_scales": wp[1],
        "us": (np.random.uniform(0.5, 1.5, (1, R)) * fr).astype(np.float32),
        "wb_words": wbp[0],
        "wb_scales": wbp[1],
        "rs": (n((N, J))).astype(np.float32),
        "offs": striped(idx),
        "offs2": striped(idx2),
    }


def reference(xf, fk, w_words, w_scales, us, wb_words, wb_scales, rs, offs, offs2):
    idx = unstriped(offs)
    idx2 = unstriped(offs2)
    wu = unpack_weight(w_words, w_scales, "e2m1")
    wbu = unpack_weight(wb_words, wb_scales, "e4m3")
    u = (f64(xf)[:, idx] - f64(xf)[:, idx2]) * f64(fk)
    uq = mxq(u, 0, "e4m3")
    a = uq.T @ wu
    m1 = np.pad(a, ((0, 0), (1, 0)))[:, :R]
    hr = (a - 0.7 * m1) * f64(us)
    hid = hr.T
    hidq = mxq(hid, 0, "e5m2")
    p = wbu.T @ hidq
    p1 = np.pad(p, ((0, 0), (1, 0)))[:, :J]
    y = p - 0.7 * p1 + 0.5 * f64(rs)
    return y

@@ -1,0 +1,218 @@
+from contextlib import ExitStack
+
+import concourse.mybir as mybir
+
+K, T, J, R, N = 512, 512, 256, 512, 256
+FLOPS = 2 * K * J * R + 2 * R * J * N
+
+F32 = mybir.dt.float32
+BF16 = mybir.dt.bfloat16
+I32 = mybir.dt.int32
+U32 = mybir.dt.uint32
+U16 = mybir.dt.uint16
+U8 = mybir.dt.uint8
+E4M3 = mybir.dt.float8_e4m3fn_x4
+E5M2 = mybir.dt.float8_e5m2_x4
+E2M1 = mybir.dt.float4_e2m1fn_x4
+MULT = mybir.AluOpType.mult
+ADD = mybir.AluOpType.add
+SUB = mybir.AluOpType.subtract
+COPY = mybir.ActivationFunctionType.Copy
+
+P = 128
+PACK = 4
+H = 128
+LAG = 0.7
+
+
+def tile_list_rows_pickgaps_neighbours_lagged_kernel(
+    tc, xf, fk, w_words, w_scales, us, wb_words, wb_scales, rs, offs, offs2, out
+):
+    nc = tc.nc
+    halves = J // H
+
+    with ExitStack() as ctx:
+        keep = ctx.enter_context(tc.tile_pool(name="keep", bufs=1))
+        psum = ctx.enter_context(tc.psum_pool(name="psum", bufs=8))
+
+        first = keep.tile([P, J // 16], U16, name="first")
+        second = keep.tile([P, J // 16], U16, name="second")
+        x = [keep.tile([P, T], F32, name=f"x{t}") for t in range(PACK)]
+        fk_sb = keep.tile([P, PACK], F32, name="fk_sb")
+        us_sb = keep.tile([P, PACK], F32, name="us_sb")
+        us_lag = keep.tile([P, PACK], F32, name="us_lag")
+        w_raw = keep.tile([P, 2 * R], U8, name="w_raw", align_bytes=64)
+        ws_raw = keep.tile([P, R], U8, name="ws_raw", align_bytes=64)
+        w_dealt = keep.tile([P, (PACK + 1) * 2 * P], U8, name="w_dealt", align_bytes=64)
+        ws_dealt = keep.tile([P, (PACK + 1) * P], U8, name="ws_dealt", align_bytes=64)
+        wb_sb = keep.tile([P, N], U32, name="wb_sb", align_bytes=64)
+        wbs_sb = keep.tile([P, N], U8, name="wbs_sb", align_bytes=64)
+        rs_sb = keep.tile([P, N // P, J], F32, name="rs_sb")
+        y = {(h, i): keep.tile([P, H], F32, name=f"y{h}{i}") for h in range(halves) for i in range(N // P)}
+
+        def load_scales(queue, tile, scales):
+            rows = scales[0].bitcast(I32)
+            for q in range(4):
+                queue.dma_start(out=tile[32 * q : 32 * q + 4, :].bitcast(I32), in_=rows[4 * q : 4 * q + 4, :])
+
+        nc.gpsimd.memset(ws_raw[:].bitcast(U32), 0)
+        x_planes = xf.rearrange("(p t) c -> p t c", t=PACK)
+        nc.sync.dma_start(out=w_raw[:].bitcast(I32), in_=w_words[0].bitcast(I32))
+        nc.sync.dma_start(second[:], offs2)
+        nc.sync.dma_start(out=x[0][:], in_=x_planes[:, 0, :])
+        nc.sync.dma_start(first[:], offs)
+        for t in range(1, PACK):
+            nc.sync.dma_start(out=x[t][:], in_=x_planes[:, t, :])
+        load_scales(nc.sync, ws_raw, w_scales)
+        nc.sync.dma_start(out=fk_sb[:], in_=fk.rearrange("(p t) o -> p (t o)", t=PACK))
+        nc.sync.dma_start(out=us_sb[:], in_=us.rearrange("o (p t) -> p (o t)", t=PACK))
+        nc.sync.dma_start(
+            out=wb_sb[:].bitcast(I32), in_=wb_words[0].rearrange("p n t -> p (n t)").bitcast(I32)
+        )
+        nc.gpsimd.memset(wbs_sb[:].bitcast(U32), 0)
+        load_scales(nc.sync, wbs_sb, wb_scales)
+        nc.sync.dma_start(out=rs_sb[:], in_=rs.rearrange("(i p) j -> p i j", p=P))
+
+        nc.gpsimd.memset(w_dealt[:, 0:4].bitcast(U32), 0)
+        nc.gpsimd.memset(ws_dealt[:, 0:4].bitcast(U32), 0)
+        w16 = w_raw[:].bitcast(U16)
+        wd16 = w_dealt[:].bitcast(U16)
+        nc.vector.tensor_copy(
+            out=wd16[:, P:].rearrange("q (t p) -> q t p", t=PACK),
+            in_=w16.rearrange("q (p t) -> q t p", t=PACK),
+        )
+        nc.vector.tensor_copy(out=wd16[:, 1:P], in_=w16[:, PACK - 1 : R - 1 : PACK])
+        nc.vector.tensor_copy(
+            out=ws_dealt[:, P:].rearrange("q (t p) -> q t p", t=PACK),
+            in_=ws_raw[:].rearrange("q (p t) -> q t p", t=PACK),
+        )
+        nc.vector.tensor_copy(out=ws_dealt[:, 1:P], in_=ws_raw[:, PACK - 1 : R - 1 : PACK])
+        nc.gpsimd.tensor_scalar(us_lag[:], us_sb[:], -LAG, 0.0, MULT, ADD)
+
+        diffs = keep.tile([P, PACK + 2, H], F32, name="diffs")
+        hid_planes = [keep.tile([P, PACK, H], BF16, name=f"hid_planes{h}") for h in range(halves)]
+        a = {}
+        banks = {}
+        u_q = {}
+        hid_q = {}
+
+        picked = keep.tile([P, 8, H], F32, name="picked")
+        slot = {(0, 0): 0, (0, 1): 1, (1, 0): 2, (1, 1): 3, (2, 0): 4, (3, 0): 6}
+
+        def entries(h):
+            return slice(h * H // 16, (h + 1) * H // 16)
+
+        def pick(dst, t, offsets, h):
+            nc.scalar.activation(picked[:, dst, :], x[t][:].indirect(offsets[:, entries(h)]), COPY)
+
+        def gap(t, h):
+            pick(slot[t, h], t, second, h)
+            nc.vector.tensor_tensor(
+                diffs[:, 2 * (1 - h) + t, :], x[t][:].indirect(first[:, entries(h)]), picked[:, slot[t, h], :], SUB
+            )
+
+        def weave_u(h):
+            woven = keep.tile([P, H, PACK], BF16, name=f"u_woven{h}", align_bytes=64)
+            lo = 2 * (1 - h)
+            nc.vector.tensor_tensor(
+                woven[:].rearrange("p (c i) t -> p c t i", i=4),
+                diffs[:, lo : lo + PACK, :].rearrange("p t (c i) -> p c t i", i=4),
+                fk_sb[:].unsqueeze(1).unsqueeze(3).broadcast_to([P, H // 4, PACK, 4]),
+                MULT,
+            )
+            return woven
+
+        def weave_hid(h):
+            woven = keep.tile([P, H, PACK], BF16, name=f"hid_woven{h}", align_bytes=64)
+            copy = nc.scalar.copy if h == 0 else nc.vector.tensor_copy
+            copy(
+                out=woven[:].rearrange("p (c i) t -> p c t i", i=4),
+                in_=hid_planes[h][:].rearrange("p t (c i) -> p c t i", i=4),
+            )
+            return woven
+
+        def quantise(woven, fmt, name):
+            codes = keep.tile([P, H], U32, name=f"{name}_codes", align_bytes=64)
+            scales = keep.tile([P, H], U8, name=f"{name}_scales", align_bytes=64)
+            nc.vector.quantize_mx(
+                out=codes[:].bitcast(fmt), scales=scales[:], in_=woven[:].rearrange("p j t -> p (j t)")
+            )
+            return codes, scales
+
+        def first_product(h):
+            codes, scales = u_q[h]
+            for s in (3, 4, 2, 1, 0):
+                if s == 0:
+                    a[h, s] = banks[h, PACK][:, 1, :]
+                else:
+                    banks[h, s] = psum.tile([P, 2, H], F32, name="bank")
+                    a[h, s] = banks[h, s][:, 0, :]
+                nc.tensor.matmul_mx(
+                    out=a[h, s],
+                    lhsT=w_dealt[:, 2 * P * s : 2 * P * (s + 1)].bitcast(E2M1),
+                    lhsT_scale=ws_dealt[:, P * s : P * (s + 1)],
+                    rhs=codes[:].bitcast(E4M3),
+                    rhs_scale=scales[:],
+                    start=True,
+                    stop=True,
+                )
+
+        def hidden(h):
+            for t in reversed(range(PACK)):
+                lagged = keep.tile([P, H], F32, name=f"lagged{t}{h}")
+                nc.scalar.activation(lagged[:], a[h, t], COPY, scale=us_lag[:, t : t + 1])
+                nc.vector.scalar_tensor_tensor(
+                    hid_planes[h][:, t, :], a[h, t + 1], us_sb[:, t : t + 1], lagged[:], MULT, ADD
+                )
+
+        def second_product(h):
+            codes, scales = hid_q[h]
+            for i in range(N // P):
+                nc.tensor.matmul_mx(
+                    out=p_bank[:, i, h * H : (h + 1) * H],
+                    lhsT=wb_sb[:, P * i : P * (i + 1)].bitcast(E4M3),
+                    lhsT_scale=wbs_sb[:, P * i : P * (i + 1)],
+                    rhs=codes[:].bitcast(E5M2),
+                    rhs_scale=scales[:],
+                    start=True,
+                    stop=True,
+                )
+
+        def finish(h):
+            lo, hi = h * H, (h + 1) * H
+            skip = 1 if h == 0 else 0
+            for i in range(N // P):
+                nc.vector.scalar_tensor_tensor(y[h, i][:], rs_sb[:, i, lo:hi], 0.5, p_bank[:, i, lo:hi], MULT, ADD)
+            for i, queue in enumerate((nc.sync, nc.scalar)):
+                nc.vector.scalar_tensor_tensor(
+                    y[h, i][:, skip:], p_bank[:, i, lo + skip - 1 : hi - 1], -LAG, y[h, i][:, skip:], MULT, ADD
+                )
+                queue.dma_start(out=out[P * i : P * (i + 1), lo:hi], in_=y[h, i][:])
+
+        gap(0, 0)
+        gap(0, 1)
+        gap(1, 0)
+        gap(1, 1)
+        gap(2, 0)
+        gap(3, 0)
+        pick(5, 3, second, 1)
+        pick(7, 3, first, 1)
+        pick(4, 2, second, 1)
+        pick(6, 2, first, 1)
+        u_woven = weave_u(0)
+        nc.vector.tensor_tensor(diffs[:, 2:4, :], picked[:, 6:8, :], picked[:, 4:6, :], SUB)
+        u_q[0] = quantise(u_woven, E4M3, "u0")
+        first_product(0)
+        u_woven = weave_u(1)
+        u_q[1] = quantise(u_woven, E4M3, "u1")
+        first_product(1)
+        p_bank = psum.tile([P, N // P, J], F32, name="bank")
+        hidden(0)
+        hid_woven = weave_hid(0)
+        hidden(1)
+        hid_q[0] = quantise(hid_woven, E5M2, "hid0")
+        second_product(0)
+        hid_q[1] = quantise(weave_hid(1), E5M2, "hid1")
+        finish(0)
+        second_product(1)
+        finish(1)

@@ -18,6 +18,7 @@ MULT = mybir.AluOpType.mult
 ADD = mybir.AluOpType.add
 SUB = mybir.AluOpType.subtract
 COPY = mybir.ActivationFunctionType.Copy
+IDENTITY = mybir.ActivationFunctionType.Identity
 
 P = 128
 PACK = 4
@@ -56,11 +57,14 @@ def tile_list_rows_pickgaps_neighbours_lagged_kernel(
                 queue.dma_start(out=tile[32 * q : 32 * q + 4, :].bitcast(I32), in_=rows[4 * q : 4 * q + 4, :])
 
         nc.gpsimd.memset(ws_raw[:].bitcast(U32), 0)
+        warm = keep.tile([P, 2], F32, name="warm")
+        nc.vector.memset(warm[:, 0:1], 0.0)
+        nc.scalar.activation(warm[:, 1:2], warm[:, 0:1], COPY)
         x_planes = xf.rearrange("(p t) c -> p t c", t=PACK)
-        nc.sync.dma_start(out=w_raw[:].bitcast(I32), in_=w_words[0].bitcast(I32))
         nc.sync.dma_start(second[:], offs2)
         nc.sync.dma_start(out=x[0][:], in_=x_planes[:, 0, :])
         nc.sync.dma_start(first[:], offs)
+        nc.sync.dma_start(out=w_raw[:].bitcast(I32), in_=w_words[0].bitcast(I32))
         for t in range(1, PACK):
             nc.sync.dma_start(out=x[t][:], in_=x_planes[:, t, :])
         load_scales(nc.sync, ws_raw, w_scales)
@@ -92,9 +96,9 @@ def tile_list_rows_pickgaps_neighbours_lagged_kernel(
         diffs = keep.tile([P, PACK + 2, H], F32, name="diffs")
         hid_planes = [keep.tile([P, PACK, H], BF16, name=f"hid_planes{h}") for h in range(halves)]
         a = {}
-        banks = {}
         u_q = {}
         hid_q = {}
+        p = {}
 
         picked = keep.tile([P, 8, H], F32, name="picked")
         slot = {(0, 0): 0, (0, 1): 1, (1, 0): 2, (1, 1): 3, (2, 0): 4, (3, 0): 6}
@@ -124,8 +128,7 @@ def tile_list_rows_pickgaps_neighbours_lagged_kernel(
 
         def weave_hid(h):
             woven = keep.tile([P, H, PACK], BF16, name=f"hid_woven{h}", align_bytes=64)
-            copy = nc.scalar.copy if h == 0 else nc.vector.tensor_copy
-            copy(
+            nc.vector.tensor_copy(
                 out=woven[:].rearrange("p (c i) t -> p c t i", i=4),
                 in_=hid_planes[h][:].rearrange("p t (c i) -> p c t i", i=4),
             )
@@ -142,13 +145,9 @@ def tile_list_rows_pickgaps_neighbours_lagged_kernel(
         def first_product(h):
             codes, scales = u_q[h]
             for s in (3, 4, 2, 1, 0):
-                if s == 0:
-                    a[h, s] = banks[h, PACK][:, 1, :]
-                else:
-                    banks[h, s] = psum.tile([P, 2, H], F32, name="bank")
-                    a[h, s] = banks[h, s][:, 0, :]
+                a[h, s] = psum.tile([P, H], F32, name="bank")
                 nc.tensor.matmul_mx(
-                    out=a[h, s],
+                    out=a[h, s][:],
                     lhsT=w_dealt[:, 2 * P * s : 2 * P * (s + 1)].bitcast(E2M1),
                     lhsT_scale=ws_dealt[:, P * s : P * (s + 1)],
                     rhs=codes[:].bitcast(E4M3),
@@ -160,16 +159,17 @@ def tile_list_rows_pickgaps_neighbours_lagged_kernel(
         def hidden(h):
             for t in reversed(range(PACK)):
                 lagged = keep.tile([P, H], F32, name=f"lagged{t}{h}")
-                nc.scalar.activation(lagged[:], a[h, t], COPY, scale=us_lag[:, t : t + 1])
+                nc.scalar.activation(lagged[:], a[h, t][:], COPY, scale=us_lag[:, t : t + 1])
                 nc.vector.scalar_tensor_tensor(
-                    hid_planes[h][:, t, :], a[h, t + 1], us_sb[:, t : t + 1], lagged[:], MULT, ADD
+                    hid_planes[h][:, t, :], a[h, t + 1][:], us_sb[:, t : t + 1], lagged[:], MULT, ADD
                 )
 
         def second_product(h):
             codes, scales = hid_q[h]
             for i in range(N // P):
+                p[h, i] = psum.tile([P, H], F32, name="bank")
                 nc.tensor.matmul_mx(
-                    out=p_bank[:, i, h * H : (h + 1) * H],
+                    out=p[h, i][:],
                     lhsT=wb_sb[:, P * i : P * (i + 1)].bitcast(E4M3),
                     lhsT_scale=wbs_sb[:, P * i : P * (i + 1)],
                     rhs=codes[:].bitcast(E5M2),
@@ -178,14 +178,18 @@ def tile_list_rows_pickgaps_neighbours_lagged_kernel(
                     stop=True,
                 )
 
+        def carry():
+            for i in range(N // P):
+                column = rs_sb[:, i, H : H + 1]
+                nc.scalar.activation(column, p[0, i][:, H - 1 : H], IDENTITY, bias=column, scale=-2 * LAG)
+
         def finish(h):
             lo, hi = h * H, (h + 1) * H
-            skip = 1 if h == 0 else 0
             for i in range(N // P):
-                nc.vector.scalar_tensor_tensor(y[h, i][:], rs_sb[:, i, lo:hi], 0.5, p_bank[:, i, lo:hi], MULT, ADD)
+                nc.vector.scalar_tensor_tensor(y[h, i][:], rs_sb[:, i, lo:hi], 0.5, p[h, i][:], MULT, ADD)
             for i, queue in enumerate((nc.sync, nc.scalar)):
                 nc.vector.scalar_tensor_tensor(
-                    y[h, i][:, skip:], p_bank[:, i, lo + skip - 1 : hi - 1], -LAG, y[h, i][:, skip:], MULT, ADD
+                    y[h, i][:, 1:], p[h, i][:, : H - 1], -LAG, y[h, i][:, 1:], MULT, ADD
                 )
                 queue.dma_start(out=out[P * i : P * (i + 1), lo:hi], in_=y[h, i][:])
 
@@ -200,19 +204,19 @@ def tile_list_rows_pickgaps_neighbours_lagged_kernel(
         pick(4, 2, second, 1)
         pick(6, 2, first, 1)
         u_woven = weave_u(0)
-        nc.vector.tensor_tensor(diffs[:, 2:4, :], picked[:, 6:8, :], picked[:, 4:6, :], SUB)
         u_q[0] = quantise(u_woven, E4M3, "u0")
+        nc.vector.tensor_tensor(diffs[:, 2:4, :], picked[:, 6:8, :], picked[:, 4:6, :], SUB)
         first_product(0)
         u_woven = weave_u(1)
         u_q[1] = quantise(u_woven, E4M3, "u1")
-        first_product(1)
-        p_bank = psum.tile([P, N // P, J], F32, name="bank")
         hidden(0)
+        first_product(1)
         hid_woven = weave_hid(0)
         hidden(1)
         hid_q[0] = quantise(hid_woven, E5M2, "hid0")
         second_product(0)
         hid_q[1] = quantise(weave_hid(1), E5M2, "hid1")
-        finish(0)
         second_product(1)
+        carry()
+        finish(0)
         finish(1)

@@ -49,7 +49,6 @@ def tile_list_rows_pickgaps_neighbours_lagged_kernel(
         wb_sb = keep.tile([P, N], U32, name="wb_sb", align_bytes=64)
         wbs_sb = keep.tile([P, N], U8, name="wbs_sb", align_bytes=64)
         rs_sb = keep.tile([P, N // P, J], F32, name="rs_sb")
-        y = {(h, i): keep.tile([P, H], F32, name=f"y{h}{i}") for h in range(halves) for i in range(N // P)}
 
         def load_scales(queue, tile, scales):
             rows = scales[0].bitcast(I32)
@@ -64,9 +63,9 @@ def tile_list_rows_pickgaps_neighbours_lagged_kernel(
         nc.sync.dma_start(second[:], offs2)
         nc.sync.dma_start(out=x[0][:], in_=x_planes[:, 0, :])
         nc.sync.dma_start(first[:], offs)
-        nc.sync.dma_start(out=w_raw[:].bitcast(I32), in_=w_words[0].bitcast(I32))
         for t in range(1, PACK):
             nc.sync.dma_start(out=x[t][:], in_=x_planes[:, t, :])
+        nc.sync.dma_start(out=w_raw[:].bitcast(I32), in_=w_words[0].bitcast(I32))
         load_scales(nc.sync, ws_raw, w_scales)
         nc.sync.dma_start(out=fk_sb[:], in_=fk.rearrange("(p t) o -> p (t o)", t=PACK))
         nc.sync.dma_start(out=us_sb[:], in_=us.rearrange("o (p t) -> p (o t)", t=PACK))
@@ -91,7 +90,7 @@ def tile_list_rows_pickgaps_neighbours_lagged_kernel(
             in_=ws_raw[:].rearrange("q (p t) -> q t p", t=PACK),
         )
         nc.vector.tensor_copy(out=ws_dealt[:, 1:P], in_=ws_raw[:, PACK - 1 : R - 1 : PACK])
-        nc.gpsimd.tensor_scalar(us_lag[:], us_sb[:], -LAG, 0.0, MULT, ADD)
+        nc.scalar.activation(us_lag[:], us_sb[:], COPY, scale=-LAG)
 
         diffs = keep.tile([P, PACK + 2, H], F32, name="diffs")
         hid_planes = [keep.tile([P, PACK, H], BF16, name=f"hid_planes{h}") for h in range(halves)]
@@ -185,13 +184,14 @@ def tile_list_rows_pickgaps_neighbours_lagged_kernel(
 
         def finish(h):
             lo, hi = h * H, (h + 1) * H
+            y = keep.tile([P, N // P, H], F32, name=f"hid_woven{1 - h}", align_bytes=64)
             for i in range(N // P):
-                nc.vector.scalar_tensor_tensor(y[h, i][:], rs_sb[:, i, lo:hi], 0.5, p[h, i][:], MULT, ADD)
+                nc.vector.scalar_tensor_tensor(y[:, i, :], rs_sb[:, i, lo:hi], 0.5, p[h, i][:], MULT, ADD)
             for i, queue in enumerate((nc.sync, nc.scalar)):
                 nc.vector.scalar_tensor_tensor(
-                    y[h, i][:, 1:], p[h, i][:, : H - 1], -LAG, y[h, i][:, 1:], MULT, ADD
+                    y[:, i, 1:], p[h, i][:, : H - 1], -LAG, y[:, i, 1:], MULT, ADD
                 )
-                queue.dma_start(out=out[P * i : P * (i + 1), lo:hi], in_=y[h, i][:])
+                queue.dma_start(out=out[P * i : P * (i + 1), lo:hi], in_=y[:, i, :])
 
         gap(0, 0)
         gap(0, 1)

from contextlib import ExitStack

import concourse.mybir as mybir

K, T, J, R, N = 512, 512, 256, 512, 256
FLOPS = 2 * K * J * R + 2 * R * J * N

F32 = mybir.dt.float32
BF16 = mybir.dt.bfloat16
I32 = mybir.dt.int32
U32 = mybir.dt.uint32
U16 = mybir.dt.uint16
U8 = mybir.dt.uint8
E4M3 = mybir.dt.float8_e4m3fn_x4
E5M2 = mybir.dt.float8_e5m2_x4
E2M1 = mybir.dt.float4_e2m1fn_x4
MULT = mybir.AluOpType.mult
ADD = mybir.AluOpType.add
SUB = mybir.AluOpType.subtract
COPY = mybir.ActivationFunctionType.Copy
IDENTITY = mybir.ActivationFunctionType.Identity

P = 128
PACK = 4
H = 128
LAG = 0.7


def tile_list_rows_pickgaps_neighbours_lagged_kernel(
    tc, xf, fk, w_words, w_scales, us, wb_words, wb_scales, rs, offs, offs2, out
):
    nc = tc.nc
    halves = J // H

    with ExitStack() as ctx:
        keep = ctx.enter_context(tc.tile_pool(name="keep", bufs=1))
        psum = ctx.enter_context(tc.psum_pool(name="psum", bufs=8))

        first = keep.tile([P, J // 16], U16, name="first")
        second = keep.tile([P, J // 16], U16, name="second")
        x = [keep.tile([P, T], F32, name=f"x{t}") for t in range(PACK)]
        fk_sb = keep.tile([P, PACK], F32, name="fk_sb")
        us_sb = keep.tile([P, PACK], F32, name="us_sb")
        us_lag = keep.tile([P, PACK], F32, name="us_lag")
        w_raw = keep.tile([P, 2 * R], U8, name="w_raw", align_bytes=64)
        ws_raw = keep.tile([P, R], U8, name="ws_raw", align_bytes=64)
        w_dealt = keep.tile([P, (PACK + 1) * 2 * P], U8, name="w_dealt", align_bytes=64)
        ws_dealt = keep.tile([P, (PACK + 1) * P], U8, name="ws_dealt", align_bytes=64)
        wb_sb = keep.tile([P, N], U32, name="wb_sb", align_bytes=64)
        wbs_sb = keep.tile([P, N], U8, name="wbs_sb", align_bytes=64)
        rs_sb = keep.tile([P, N // P, J], F32, name="rs_sb")

        def load_scales(queue, tile, scales):
            rows = scales[0].bitcast(I32)
            for q in range(4):
                queue.dma_start(out=tile[32 * q : 32 * q + 4, :].bitcast(I32), in_=rows[4 * q : 4 * q + 4, :])

        nc.gpsimd.memset(ws_raw[:].bitcast(U32), 0)
        warm = keep.tile([P, 2], F32, name="warm")
        nc.vector.memset(warm[:, 0:1], 0.0)
        nc.scalar.activation(warm[:, 1:2], warm[:, 0:1], COPY)
        x_planes = xf.rearrange("(p t) c -> p t c", t=PACK)
        nc.sync.dma_start(second[:], offs2)
        nc.sync.dma_start(out=x[0][:], in_=x_planes[:, 0, :])
        nc.sync.dma_start(first[:], offs)
        for t in range(1, PACK):
            nc.sync.dma_start(out=x[t][:], in_=x_planes[:, t, :])
        nc.sync.dma_start(out=w_raw[:].bitcast(I32), in_=w_words[0].bitcast(I32))
        load_scales(nc.sync, ws_raw, w_scales)
        nc.sync.dma_start(out=fk_sb[:], in_=fk.rearrange("(p t) o -> p (t o)", t=PACK))
        nc.sync.dma_start(out=us_sb[:], in_=us.rearrange("o (p t) -> p (o t)", t=PACK))
        nc.sync.dma_start(
            out=wb_sb[:].bitcast(I32), in_=wb_words[0].rearrange("p n t -> p (n t)").bitcast(I32)
        )
        nc.gpsimd.memset(wbs_sb[:].bitcast(U32), 0)
        load_scales(nc.sync, wbs_sb, wb_scales)
        nc.sync.dma_start(out=rs_sb[:], in_=rs.rearrange("(i p) j -> p i j", p=P))

        nc.gpsimd.memset(w_dealt[:, 0:4].bitcast(U32), 0)
        nc.gpsimd.memset(ws_dealt[:, 0:4].bitcast(U32), 0)
        w16 = w_raw[:].bitcast(U16)
        wd16 = w_dealt[:].bitcast(U16)
        nc.vector.tensor_copy(
            out=wd16[:, P:].rearrange("q (t p) -> q t p", t=PACK),
            in_=w16.rearrange("q (p t) -> q t p", t=PACK),
        )
        nc.vector.tensor_copy(out=wd16[:, 1:P], in_=w16[:, PACK - 1 : R - 1 : PACK])
        nc.vector.tensor_copy(
            out=ws_dealt[:, P:].rearrange("q (t p) -> q t p", t=PACK),
            in_=ws_raw[:].rearrange("q (p t) -> q t p", t=PACK),
        )
        nc.vector.tensor_copy(out=ws_dealt[:, 1:P], in_=ws_raw[:, PACK - 1 : R - 1 : PACK])
        nc.scalar.activation(us_lag[:], us_sb[:], COPY, scale=-LAG)

        diffs = keep.tile([P, PACK + 2, H], F32, name="diffs")
        hid_planes = [keep.tile([P, PACK, H], BF16, name=f"hid_planes{h}") for h in range(halves)]
        a = {}
        u_q = {}
        hid_q = {}
        p = {}

        picked = keep.tile([P, 8, H], F32, name="picked")
        slot = {(0, 0): 0, (0, 1): 1, (1, 0): 2, (1, 1): 3, (2, 0): 4, (3, 0): 6}

        def entries(h):
            return slice(h * H // 16, (h + 1) * H // 16)

        def pick(dst, t, offsets, h):
            nc.scalar.activation(picked[:, dst, :], x[t][:].indirect(offsets[:, entries(h)]), COPY)

        def gap(t, h):
            pick(slot[t, h], t, second, h)
            nc.vector.tensor_tensor(
                diffs[:, 2 * (1 - h) + t, :], x[t][:].indirect(first[:, entries(h)]), picked[:, slot[t, h], :], SUB
            )

        def weave_u(h):
            woven = keep.tile([P, H, PACK], BF16, name=f"u_woven{h}", align_bytes=64)
            lo = 2 * (1 - h)
            nc.vector.tensor_tensor(
                woven[:].rearrange("p (c i) t -> p c t i", i=4),
                diffs[:, lo : lo + PACK, :].rearrange("p t (c i) -> p c t i", i=4),
                fk_sb[:].unsqueeze(1).unsqueeze(3).broadcast_to([P, H // 4, PACK, 4]),
                MULT,
            )
            return woven

        def weave_hid(h):
            woven = keep.tile([P, H, PACK], BF16, name=f"hid_woven{h}", align_bytes=64)
            nc.vector.tensor_copy(
                out=woven[:].rearrange("p (c i) t -> p c t i", i=4),
                in_=hid_planes[h][:].rearrange("p t (c i) -> p c t i", i=4),
            )
            return woven

        def quantise(woven, fmt, name):
            codes = keep.tile([P, H], U32, name=f"{name}_codes", align_bytes=64)
            scales = keep.tile([P, H], U8, name=f"{name}_scales", align_bytes=64)
            nc.vector.quantize_mx(
                out=codes[:].bitcast(fmt), scales=scales[:], in_=woven[:].rearrange("p j t -> p (j t)")
            )
            return codes, scales

        def first_product(h):
            codes, scales = u_q[h]
            for s in (3, 4, 2, 1, 0):
                a[h, s] = psum.tile([P, H], F32, name="bank")
                nc.tensor.matmul_mx(
                    out=a[h, s][:],
                    lhsT=w_dealt[:, 2 * P * s : 2 * P * (s + 1)].bitcast(E2M1),
                    lhsT_scale=ws_dealt[:, P * s : P * (s + 1)],
                    rhs=codes[:].bitcast(E4M3),
                    rhs_scale=scales[:],
                    start=True,
                    stop=True,
                )

        def hidden(h):
            for t in reversed(range(PACK)):
                lagged = keep.tile([P, H], F32, name=f"lagged{t}{h}")
                nc.scalar.activation(lagged[:], a[h, t][:], COPY, scale=us_lag[:, t : t + 1])
                nc.vector.scalar_tensor_tensor(
                    hid_planes[h][:, t, :], a[h, t + 1][:], us_sb[:, t : t + 1], lagged[:], MULT, ADD
                )

        def second_product(h):
            codes, scales = hid_q[h]
            for i in range(N // P):
                p[h, i] = psum.tile([P, H], F32, name="bank")
                nc.tensor.matmul_mx(
                    out=p[h, i][:],
                    lhsT=wb_sb[:, P * i : P * (i + 1)].bitcast(E4M3),
                    lhsT_scale=wbs_sb[:, P * i : P * (i + 1)],
                    rhs=codes[:].bitcast(E5M2),
                    rhs_scale=scales[:],
                    start=True,
                    stop=True,
                )

        def carry():
            for i in range(N // P):
                column = rs_sb[:, i, H : H + 1]
                nc.scalar.activation(column, p[0, i][:, H - 1 : H], IDENTITY, bias=column, scale=-2 * LAG)

        def finish(h):
            lo, hi = h * H, (h + 1) * H
            y = keep.tile([P, N // P, H], F32, name=f"hid_woven{1 - h}", align_bytes=64)
            for i in range(N // P):
                nc.vector.scalar_tensor_tensor(y[:, i, :], rs_sb[:, i, lo:hi], 0.5, p[h, i][:], MULT, ADD)
            for i, queue in enumerate((nc.sync, nc.scalar)):
                nc.vector.scalar_tensor_tensor(
                    y[:, i, 1:], p[h, i][:, : H - 1], -LAG, y[:, i, 1:], MULT, ADD
                )
                queue.dma_start(out=out[P * i : P * (i + 1), lo:hi], in_=y[:, i, :])

        gap(0, 0)
        gap(0, 1)
        gap(1, 0)
        gap(1, 1)
        gap(2, 0)
        gap(3, 0)
        pick(5, 3, second, 1)
        pick(7, 3, first, 1)
        pick(4, 2, second, 1)
        pick(6, 2, first, 1)
        u_woven = weave_u(0)
        u_q[0] = quantise(u_woven, E4M3, "u0")
        nc.vector.tensor_tensor(diffs[:, 2:4, :], picked[:, 6:8, :], picked[:, 4:6, :], SUB)
        first_product(0)
        u_woven = weave_u(1)
        u_q[1] = quantise(u_woven, E4M3, "u1")
        hidden(0)
        first_product(1)
        hid_woven = weave_hid(0)
        hidden(1)
        hid_q[0] = quantise(hid_woven, E5M2, "hid0")
        second_product(0)
        hid_q[1] = quantise(weave_hid(1), E5M2, "hid1")
        second_product(1)
        carry()
        finish(0)
        finish(1)
